import numpy as np
import ml_dtypes


def mxq(x, axis, fmt="e4m3"):
    dtype, down = {"e4m3": (ml_dtypes.float8_e4m3fn, 7), "e5m2": (ml_dtypes.float8_e5m2, 14)}[fmt]
    v = np.moveaxis(np.asarray(x, np.float32).astype(ml_dtypes.bfloat16).astype(np.float64), axis, -1)
    blocks = v.reshape(v.shape[:-1] + (-1, 32))
    amax = np.abs(blocks).max(-1, keepdims=True)
    byte = np.maximum(np.where(amax > 0, np.frexp(amax)[1] - 1 + 127, 0) - down, 1)
    scale = np.exp2(byte - 127.0)
    codes = (blocks / scale).astype(np.float32).astype(dtype).astype(np.float64)
    return np.moveaxis((codes * scale).reshape(v.shape), -1, axis)


WIDE = False


def mx_kscale(k):
    if not WIDE:
        return np.ones(k)
    levels = np.array([10, -10, 5, -5, 0])
    if k % 512:
        return np.exp2(np.random.permutation(np.resize(levels, k // 32))).repeat(32)
    a = np.empty((k // 512, 16))
    for p in range(k // 512):
        a[p, :8] = np.random.permutation(np.resize(levels, 8))
        for g in range(8):
            far = levels[np.abs(levels - a[p, g]) >= 10]
            a[p, g + 8] = far[np.random.randint(len(far))]
    return np.exp2(a.ravel()).repeat(32)


def f64(x):
    return np.asarray(x).astype(np.float64)


def striped8(idx):
    return np.asarray(idx).reshape(8, -1, 16).transpose(0, 2, 1).reshape(128, -1).astype(np.uint16)


def unstriped8(offs):
    return offs.reshape(8, 16, -1).transpose(0, 2, 1).reshape(8, -1).astype(np.int64)


def pick8(x, idx, run):
    r = np.arange(len(x))
    return x[r[:, None], idx[r % (8 * run) // run]]


E2M1 = np.array([0.0, 0.5, 1.0, 1.5, 2.0, 3.0, 4.0, 6.0, -0.0, -0.5, -1.0, -1.5, -2.0, -3.0, -4.0, -6.0])


def pack_weight(w, fmt):
    k, n = w.shape
    w = f64(np.asarray(w, np.float32).astype(ml_dtypes.bfloat16)).reshape(k // 32, 32, n)
    amax = np.abs(w).max(1)
    if fmt == "e4m3":
        byte = np.frexp(amax)[1] - 1 + 127 - 7
    else:
        mant, ex = np.frexp(amax / 6.0)
        byte = np.where(mant > 0.5, ex, ex - 1) + 127
    byte = np.clip(np.where(amax > 0, byte, 1), 1, 254)
    scaled = (w * np.exp2(127.0 - byte)[:, None, :]).reshape(k, n).astype(np.float32)
    by_word = np.ascontiguousarray(scaled.reshape(k // 512, 128, 4, n).transpose(0, 1, 3, 2))
    if fmt == "e4m3":
        words = by_word.astype(ml_dtypes.float8_e4m3fn).view(np.uint8)
    else:
        c = by_word.astype(ml_dtypes.float4_e2m1fn).view(np.uint8) & 0xF
        words = (c[..., 0::2] | (c[..., 1::2] << 4)).reshape(k // 512, 128, 2 * n)
    return np.ascontiguousarray(words), np.ascontiguousarray(byte.astype(np.uint8).reshape(k // 512, 16, n))


def unpack_weight(words, scales, fmt):
    g, _, n = scales.shape
    words = np.ascontiguousarray(words).reshape(g, 128, n, -1)
    if fmt == "e4m3":
        vals = words.view(ml_dtypes.float8_e4m3fn).astype(np.float64)
    else:
        nib = np.empty((g, 128, n, 4), np.uint8)
        nib[..., 0::2] = words & 0xF
        nib[..., 1::2] = words >> 4
        vals = E2M1[nib]
    vals = vals * np.repeat(np.exp2(scales.astype(np.float64) - 127.0), 8, axis=1)[..., None]
    return vals.transpose(0, 1, 3, 2).reshape(g * 512, n)


def softplus(v):
    return np.log(1.0 + np.exp(v))


D, T, I, Q = 512, 1024, 512, 128


def setup_inputs():
    n = np.random.standard_normal
    idx = np.stack([np.random.permutation(T)[:I] for _ in range(8)])
    fd = mx_kscale(D)
    keysp = pack_weight(n((D, T)) / fd[:, None], "e4m3")
    return {
        "query": (n((D, Q)) * 0.9 / np.sqrt(D) * fd[:, None]).astype(np.float32),
        "query2": (n((D, Q)) * 0.9 / np.sqrt(D) * fd[:, None]).astype(np.float32),
        "keys_words": keysp[0],
        "keys_scales": keysp[1],
        "lam": (np.random.uniform(1.0, 2.0, (Q, 1))).astype(np.float32),
        "old": (np.random.uniform(0.0, 2.0, (Q, T))).astype(np.float32),
        "fade": (np.random.uniform(0.3, 0.9, (Q, 1))).astype(np.float32),
        "offs": striped8(idx),
    }


def reference(query, query2, keys_words, keys_scales, lam, old, fade, offs):
    idx = unstriped8(offs)
    keysu = unpack_weight(keys_words, keys_scales, "e4m3")
    queryq = mxq(f64(query), 0, "e4m3")
    a = queryq.T @ keysu
    query2q = mxq(f64(query2), 0, "e4m3")
    b = query2q.T @ keysu
    ra = np.sqrt(softplus(pick8(a, idx, 16)) * softplus(pick8(b, idx, 16)) + 0.1)
    s = ra * f64(lam) - np.abs(pick8(a, idx, 16) - pick8(b, idx, 16))
    p = np.exp(s - np.max(s, axis=1, keepdims=True))
    w = p / np.sum(p, axis=1, keepdims=True)
    ws = w * 256.0
    wf = np.zeros((Q, T))
    wf[np.arange(Q)[:, None], idx[np.arange(Q) % 128 // 16]] = ws
    y = f64(old) * f64(fade) + wf
    return y

@@ -1,0 +1,170 @@
+from contextlib import ExitStack
+
+import concourse.mybir as mybir
+
+D, T, I, Q = 512, 1024, 512, 128
+FLOPS = 2 * 2 * D * Q * T
+
+F32 = mybir.dt.float32
+BF16 = mybir.dt.bfloat16
+I32 = mybir.dt.int32
+U32 = mybir.dt.uint32
+U16 = mybir.dt.uint16
+U8 = mybir.dt.uint8
+FP8X4 = mybir.dt.float8_e4m3fn_x4
+ALU = mybir.AluOpType
+ACT = mybir.ActivationFunctionType
+
+P = 128
+PACK = 4
+N_PASS = 256
+HALF = I // 2
+STORE_COLS = 256
+LN_FLOOR = 2.0 ** -62
+
+
+def tile_attend_agreeingtwo_soft_counts_heads_kernel(
+    tc, query, query2, keys_words, keys_scales, lam, old, fade, offs, out
+):
+    nc = tc.nc
+    with ExitStack() as ctx:
+        sb = ctx.enter_context(tc.tile_pool(name="sb", bufs=1))
+        ps = ctx.enter_context(tc.psum_pool(name="ps", bufs=1))
+
+        offsets = sb.tile([P, I // 16], U16, name="offsets")
+        k_scales = sb.tile([P, T], U8, name="k_scales", align_bytes=64)
+        k_words = sb.tile([P, T], U32, name="k_words", align_bytes=64)
+        q_raw = [sb.tile([P, PACK, Q], F32, name="q_raw%d" % j, tag="q_raw%d" % j) for j in range(2)]
+        q_bf = [sb.tile([P, Q, PACK], BF16, name="q_bf%d" % j, tag="q_bf%d" % j, align_bytes=64) for j in range(2)]
+        q_words = [sb.tile([P, Q], U32, name="q_words%d" % j, align_bytes=64) for j in range(2)]
+        q_scales = [sb.tile([P, Q], U8, name="q_scales%d" % j, align_bytes=64) for j in range(2)]
+        scores = [sb.tile([P, T], F32, name="scores%d" % j, tag="scores%d" % j) for j in range(2)]
+        wf = sb.tile([P, T], F32, name="wf")
+
+        nc.vector.memset(k_scales[:].bitcast(I32), 0)
+        nc.vector.memset(wf[:], 0.0)
+
+        words_hbm = keys_words[0].rearrange("p n t -> p (n t)")
+
+        def load_query(j, src):
+            nc.sync.dma_start(out=q_raw[j][:], in_=src.rearrange("(p r) w -> p r w", r=PACK))
+
+        def load_words(h):
+            c0, c1 = h * (T // 2), (h + 1) * (T // 2)
+            nc.sync.dma_start(
+                out=k_words[:, c0:c1].bitcast(I32),
+                in_=words_hbm[:, PACK * c0 : PACK * c1].bitcast(I32),
+            )
+
+        load_query(0, query)
+        for quad in range(4):
+            nc.scalar.dma_start(
+                out=k_scales[32 * quad : 32 * quad + 4, :].bitcast(I32),
+                in_=keys_scales[0, 4 * quad : 4 * quad + 4, :].bitcast(I32),
+            )
+        load_words(0)
+        load_query(1, query2)
+        load_words(1)
+        nc.sync.dma_start(offsets[:], offs)
+
+        def interleave_views(j):
+            dst = q_bf[j][:].rearrange("p (c i) r -> p c r i", i=4)
+            src = q_raw[j][:].rearrange("p r (c i) -> p c r i", i=4)
+            return dst, src
+
+        def quantize(j):
+            nc.vector.quantize_mx(
+                out=q_words[j][:].bitcast(FP8X4),
+                scales=q_scales[j][:],
+                in_=q_bf[j][:].rearrange("p w r -> p (w r)"),
+            )
+
+        nc.vector.tensor_copy(*interleave_views(0))
+        old_sb = sb.tile([P, T], F32, name="old_sb", tag="q_raw0")
+        nc.sync.dma_start(out=old_sb[:], in_=old)
+        quantize(0)
+        nc.scalar.copy(*interleave_views(1))
+        quantize(1)
+        lam_sb = sb.tile([P, 1], F32, name="lam_sb", tag="q_bf0", align_bytes=64)
+        nc.sync.dma_start(out=lam_sb[:], in_=lam)
+        fade_sb = sb.tile([P, 1], F32, name="fade_sb", tag="q_bf1", align_bytes=64)
+        nc.sync.dma_start(out=fade_sb[:], in_=fade)
+
+        copy_out = (nc.scalar.copy, nc.vector.tensor_copy)
+        for j in range(2):
+            for c0 in range(0, T, N_PASS):
+                cols = slice(c0, c0 + N_PASS)
+                acc = ps.tile([P, N_PASS], F32, name="acc%d_%d" % (j, c0))
+                nc.tensor.matmul_mx(
+                    out=acc[:],
+                    lhsT=q_words[j][:].bitcast(FP8X4),
+                    lhsT_scale=q_scales[j][:],
+                    rhs=k_words[:, cols].bitcast(FP8X4),
+                    rhs_scale=k_scales[:, cols],
+                    start=True,
+                    stop=True,
+                )
+                copy_out[j](scores[j][:, cols], acc[:])
+
+        sig = sb.tile([P, 2, I], F32, name="sig")
+        picked_b = sb.tile([P, I], F32, name="picked_b")
+        halves = [slice(h * HALF, (h + 1) * HALF) for h in range(2)]
+        off_halves = [offsets[:, h * HALF // 16 : (h + 1) * HALF // 16] for h in range(2)]
+        nc.scalar.activation(
+            sig[:, 0, :], scores[0][:].indirect(offsets[:]), ACT.Sigmoid, scale=-1.0
+        )
+        for h in range(2):
+            nc.vector.tensor_copy(picked_b[:, halves[h]], scores[1][:].indirect(off_halves[h]))
+        nc.scalar.activation(
+            sig[:, 1, halves[1]], scores[1][:].indirect(off_halves[1]), ACT.Sigmoid, scale=-1.0
+        )
+        nc.scalar.activation(sig[:, 1, halves[0]], picked_b[:, halves[0]], ACT.Sigmoid, scale=-1.0)
+        picked_a = sb.tile([P, I], F32, name="picked_a", tag="scores1")
+        nc.vector.tensor_copy(picked_a[:], scores[0][:].indirect(offsets[:]))
+        picked = (picked_a, picked_b)
+
+        logsig = sb.tile([P, 2, I], F32, name="logsig")
+        negsp = sb.tile([P, 2, I], F32, name="negsp", tag="negsp")
+        prod = sb.tile([P, I], F32, name="prod")
+        for hs in halves:
+            nc.scalar.activation(logsig[:, :, hs], sig[:, :, hs], ACT.Ln, bias=LN_FLOOR)
+        for hs in halves:
+            for j in range(2):
+                nc.vector.scalar_tensor_tensor(
+                    negsp[:, j, hs], picked[j][:, hs], -1.0, logsig[:, j, hs], ALU.mult, ALU.min
+                )
+        for hs in halves:
+            nc.vector.tensor_tensor(prod[:, hs], negsp[:, 0, hs], negsp[:, 1, hs], ALU.mult)
+
+        diff = sb.tile([P, I], F32, name="diff")
+        nc.vector.tensor_tensor(diff[:], picked_a[:], picked_b[:], ALU.subtract)
+        absdiff = sb.tile([P, I], F32, name="absdiff", tag="negsp")
+        nc.vector.scalar_tensor_tensor(absdiff[:], diff[:], -1.0, diff[:], ALU.mult, ALU.max)
+
+        root = sb.tile([P, I], F32, name="root")
+        score = sb.tile([P, I], F32, name="score")
+        for hs in halves:
+            nc.scalar.activation(root[:, hs], prod[:, hs], ACT.Sqrt, bias=0.1)
+        for hs in halves:
+            nc.vector.scalar_tensor_tensor(
+                score[:, hs], root[:, hs], lam_sb[:], absdiff[:, hs], ALU.mult, ALU.subtract
+            )
+        negmax = sb.tile([P, 1], F32, name="negmax")
+        nc.vector.tensor_reduce(negmax[:], score[:], mybir.AxisListType.X, ALU.max, negate=True)
+        prob = sb.tile([P, I], F32, name="prob")
+        total = sb.tile([P, 1], F32, name="total")
+        nc.scalar.activation(prob[:], score[:], ACT.Exp, bias=negmax[:], accum_out=total[:])
+        inv = sb.tile([P, 1], F32, name="inv")
+        nc.vector.reciprocal(inv[:], total[:])
+        ws = sb.tile([P, I], F32, name="ws")
+        nc.vector.tensor_scalar(ws[:], prob[:], inv[:], 256.0, ALU.mult, ALU.mult)
+        nc.vector.tensor_copy(wf[:].indirect(offsets[:]), ws[:])
+
+        result = sb.tile([P, T], F32, name="result")
+        queues = (nc.sync, nc.scalar)
+        for n, c0 in enumerate(range(0, T, STORE_COLS)):
+            cols = slice(c0, c0 + STORE_COLS)
+            nc.vector.scalar_tensor_tensor(
+                result[:, cols], old_sb[:, cols], fade_sb[:], wf[:, cols], ALU.mult, ALU.add
+            )
+            queues[n % 2].dma_start(out=out[:, cols], in_=result[:, cols])

@@ -42,6 +42,8 @@ def tile_attend_agreeingtwo_soft_counts_heads_kernel(
         wf = sb.tile([P, T], F32, name="wf")
 
         nc.vector.memset(k_scales[:].bitcast(I32), 0)
+        warm_in = sb.tile([P, 1], F32, name="warm_in")
+        nc.vector.memset(warm_in[:], 0.0)
         nc.vector.memset(wf[:], 0.0)
 
         words_hbm = keys_words[0].rearrange("p n t -> p (n t)")
@@ -62,6 +64,8 @@ def tile_attend_agreeingtwo_soft_counts_heads_kernel(
                 out=k_scales[32 * quad : 32 * quad + 4, :].bitcast(I32),
                 in_=keys_scales[0, 4 * quad : 4 * quad + 4, :].bitcast(I32),
             )
+        warm_out = sb.tile([P, 1], F32, name="warm_out")
+        nc.scalar.activation(warm_out[:], warm_in[:], ACT.Sigmoid)
         load_words(0)
         load_query(1, query2)
         load_words(1)

@@ -19,7 +19,7 @@ P = 128
 PACK = 4
 N_PASS = 256
 HALF = I // 2
-STORE_COLS = 256
+STORE_EDGES = (0, 256, 512, 768, 1024)
 LN_FLOOR = 2.0 ** -62
 
 
@@ -60,7 +60,7 @@ def tile_attend_agreeingtwo_soft_counts_heads_kernel(
 
         load_query(0, query)
         for quad in range(4):
-            nc.scalar.dma_start(
+            nc.sync.dma_start(
                 out=k_scales[32 * quad : 32 * quad + 4, :].bitcast(I32),
                 in_=keys_scales[0, 4 * quad : 4 * quad + 4, :].bitcast(I32),
             )
@@ -87,14 +87,13 @@ def tile_attend_agreeingtwo_soft_counts_heads_kernel(
         old_sb = sb.tile([P, T], F32, name="old_sb", tag="q_raw0")
         nc.sync.dma_start(out=old_sb[:], in_=old)
         quantize(0)
-        nc.scalar.copy(*interleave_views(1))
+        nc.vector.tensor_copy(*interleave_views(1))
         quantize(1)
         lam_sb = sb.tile([P, 1], F32, name="lam_sb", tag="q_bf0", align_bytes=64)
         nc.sync.dma_start(out=lam_sb[:], in_=lam)
         fade_sb = sb.tile([P, 1], F32, name="fade_sb", tag="q_bf1", align_bytes=64)
         nc.sync.dma_start(out=fade_sb[:], in_=fade)
 
-        copy_out = (nc.scalar.copy, nc.vector.tensor_copy)
         for j in range(2):
             for c0 in range(0, T, N_PASS):
                 cols = slice(c0, c0 + N_PASS)
@@ -108,7 +107,9 @@ def tile_attend_agreeingtwo_soft_counts_heads_kernel(
                     start=True,
                     stop=True,
                 )
-                copy_out[j](scores[j][:, cols], acc[:])
+                on_scalar = j == 0 and c0 + N_PASS < T
+                copy_out = nc.scalar.copy if on_scalar else nc.vector.tensor_copy
+                copy_out(scores[j][:, cols], acc[:])
 
         sig = sb.tile([P, 2, I], F32, name="sig")
         picked_b = sb.tile([P, I], F32, name="picked_b")
@@ -166,8 +167,8 @@ def tile_attend_agreeingtwo_soft_counts_heads_kernel(
 
         result = sb.tile([P, T], F32, name="result")
         queues = (nc.sync, nc.scalar)
-        for n, c0 in enumerate(range(0, T, STORE_COLS)):
-            cols = slice(c0, c0 + STORE_COLS)
+        for n in range(len(STORE_EDGES) - 1):
+            cols = slice(STORE_EDGES[n], STORE_EDGES[n + 1])
             nc.vector.scalar_tensor_tensor(
                 result[:, cols], old_sb[:, cols], fade_sb[:], wf[:, cols], ALU.mult, ALU.add
             )

@@ -59,6 +59,7 @@ def tile_attend_agreeingtwo_soft_counts_heads_kernel(
             )
 
         load_query(0, query)
+        load_words(0)
         for quad in range(4):
             nc.sync.dma_start(
                 out=k_scales[32 * quad : 32 * quad + 4, :].bitcast(I32),
@@ -66,7 +67,6 @@ def tile_attend_agreeingtwo_soft_counts_heads_kernel(
             )
         warm_out = sb.tile([P, 1], F32, name="warm_out")
         nc.scalar.activation(warm_out[:], warm_in[:], ACT.Sigmoid)
-        load_words(0)
         load_query(1, query2)
         load_words(1)
         nc.sync.dma_start(offsets[:], offs)

@@ -71,10 +71,11 @@ def tile_attend_agreeingtwo_soft_counts_heads_kernel(
         load_words(1)
         nc.sync.dma_start(offsets[:], offs)
 
-        def interleave_views(j):
-            dst = q_bf[j][:].rearrange("p (c i) r -> p c r i", i=4)
-            src = q_raw[j][:].rearrange("p r (c i) -> p c r i", i=4)
-            return dst, src
+        def interleave(copy, j, w0, w1):
+            copy(
+                q_bf[j][:, w0:w1, :].rearrange("p (c i) r -> p c r i", i=4),
+                q_raw[j][:, :, w0:w1].rearrange("p r (c i) -> p c r i", i=4),
+            )
 
         def quantize(j):
             nc.vector.quantize_mx(
@@ -83,11 +84,12 @@ def tile_attend_agreeingtwo_soft_counts_heads_kernel(
                 in_=q_bf[j][:].rearrange("p w r -> p (w r)"),
             )
 
-        nc.vector.tensor_copy(*interleave_views(0))
+        interleave(nc.vector.tensor_copy, 0, 0, Q // 2)
+        interleave(nc.scalar.copy, 0, Q // 2, Q)
         old_sb = sb.tile([P, T], F32, name="old_sb", tag="q_raw0")
         nc.sync.dma_start(out=old_sb[:], in_=old)
         quantize(0)
-        nc.vector.tensor_copy(*interleave_views(1))
+        interleave(nc.vector.tensor_copy, 1, 0, Q)
         quantize(1)
         lam_sb = sb.tile([P, 1], F32, name="lam_sb", tag="q_bf0", align_bytes=64)
         nc.sync.dma_start(out=lam_sb[:], in_=lam)

from contextlib import ExitStack

import concourse.mybir as mybir

D, T, I, Q = 512, 1024, 512, 128
FLOPS = 2 * 2 * D * Q * T

F32 = mybir.dt.float32
BF16 = mybir.dt.bfloat16
I32 = mybir.dt.int32
U32 = mybir.dt.uint32
U16 = mybir.dt.uint16
U8 = mybir.dt.uint8
FP8X4 = mybir.dt.float8_e4m3fn_x4
ALU = mybir.AluOpType
ACT = mybir.ActivationFunctionType

P = 128
PACK = 4
N_PASS = 256
HALF = I // 2
STORE_EDGES = (0, 256, 512, 768, 1024)
LN_FLOOR = 2.0 ** -62


def tile_attend_agreeingtwo_soft_counts_heads_kernel(
    tc, query, query2, keys_words, keys_scales, lam, old, fade, offs, out
):
    nc = tc.nc
    with ExitStack() as ctx:
        sb = ctx.enter_context(tc.tile_pool(name="sb", bufs=1))
        ps = ctx.enter_context(tc.psum_pool(name="ps", bufs=1))

        offsets = sb.tile([P, I // 16], U16, name="offsets")
        k_scales = sb.tile([P, T], U8, name="k_scales", align_bytes=64)
        k_words = sb.tile([P, T], U32, name="k_words", align_bytes=64)
        q_raw = [sb.tile([P, PACK, Q], F32, name="q_raw%d" % j, tag="q_raw%d" % j) for j in range(2)]
        q_bf = [sb.tile([P, Q, PACK], BF16, name="q_bf%d" % j, tag="q_bf%d" % j, align_bytes=64) for j in range(2)]
        q_words = [sb.tile([P, Q], U32, name="q_words%d" % j, align_bytes=64) for j in range(2)]
        q_scales = [sb.tile([P, Q], U8, name="q_scales%d" % j, align_bytes=64) for j in range(2)]
        scores = [sb.tile([P, T], F32, name="scores%d" % j, tag="scores%d" % j) for j in range(2)]
        wf = sb.tile([P, T], F32, name="wf")

        nc.vector.memset(k_scales[:].bitcast(I32), 0)
        warm_in = sb.tile([P, 1], F32, name="warm_in")
        nc.vector.memset(warm_in[:], 0.0)
        nc.vector.memset(wf[:], 0.0)

        words_hbm = keys_words[0].rearrange("p n t -> p (n t)")

        def load_query(j, src):
            nc.sync.dma_start(out=q_raw[j][:], in_=src.rearrange("(p r) w -> p r w", r=PACK))

        def load_words(h):
            c0, c1 = h * (T // 2), (h + 1) * (T // 2)
            nc.sync.dma_start(
                out=k_words[:, c0:c1].bitcast(I32),
                in_=words_hbm[:, PACK * c0 : PACK * c1].bitcast(I32),
            )

        load_query(0, query)
        load_words(0)
        for quad in range(4):
            nc.sync.dma_start(
                out=k_scales[32 * quad : 32 * quad + 4, :].bitcast(I32),
                in_=keys_scales[0, 4 * quad : 4 * quad + 4, :].bitcast(I32),
            )
        warm_out = sb.tile([P, 1], F32, name="warm_out")
        nc.scalar.activation(warm_out[:], warm_in[:], ACT.Sigmoid)
        load_query(1, query2)
        load_words(1)
        nc.sync.dma_start(offsets[:], offs)

        def interleave(copy, j, w0, w1):
            copy(
                q_bf[j][:, w0:w1, :].rearrange("p (c i) r -> p c r i", i=4),
                q_raw[j][:, :, w0:w1].rearrange("p r (c i) -> p c r i", i=4),
            )

        def quantize(j):
            nc.vector.quantize_mx(
                out=q_words[j][:].bitcast(FP8X4),
                scales=q_scales[j][:],
                in_=q_bf[j][:].rearrange("p w r -> p (w r)"),
            )

        interleave(nc.vector.tensor_copy, 0, 0, Q // 2)
        interleave(nc.scalar.copy, 0, Q // 2, Q)
        old_sb = sb.tile([P, T], F32, name="old_sb", tag="q_raw0")
        nc.sync.dma_start(out=old_sb[:], in_=old)
        quantize(0)
        interleave(nc.vector.tensor_copy, 1, 0, Q)
        quantize(1)
        lam_sb = sb.tile([P, 1], F32, name="lam_sb", tag="q_bf0", align_bytes=64)
        nc.sync.dma_start(out=lam_sb[:], in_=lam)
        fade_sb = sb.tile([P, 1], F32, name="fade_sb", tag="q_bf1", align_bytes=64)
        nc.sync.dma_start(out=fade_sb[:], in_=fade)

        for j in range(2):
            for c0 in range(0, T, N_PASS):
                cols = slice(c0, c0 + N_PASS)
                acc = ps.tile([P, N_PASS], F32, name="acc%d_%d" % (j, c0))
                nc.tensor.matmul_mx(
                    out=acc[:],
                    lhsT=q_words[j][:].bitcast(FP8X4),
                    lhsT_scale=q_scales[j][:],
                    rhs=k_words[:, cols].bitcast(FP8X4),
                    rhs_scale=k_scales[:, cols],
                    start=True,
                    stop=True,
                )
                on_scalar = j == 0 and c0 + N_PASS < T
                copy_out = nc.scalar.copy if on_scalar else nc.vector.tensor_copy
                copy_out(scores[j][:, cols], acc[:])

        sig = sb.tile([P, 2, I], F32, name="sig")
        picked_b = sb.tile([P, I], F32, name="picked_b")
        halves = [slice(h * HALF, (h + 1) * HALF) for h in range(2)]
        off_halves = [offsets[:, h * HALF // 16 : (h + 1) * HALF // 16] for h in range(2)]
        nc.scalar.activation(
            sig[:, 0, :], scores[0][:].indirect(offsets[:]), ACT.Sigmoid, scale=-1.0
        )
        for h in range(2):
            nc.vector.tensor_copy(picked_b[:, halves[h]], scores[1][:].indirect(off_halves[h]))
        nc.scalar.activation(
            sig[:, 1, halves[1]], scores[1][:].indirect(off_halves[1]), ACT.Sigmoid, scale=-1.0
        )
        nc.scalar.activation(sig[:, 1, halves[0]], picked_b[:, halves[0]], ACT.Sigmoid, scale=-1.0)
        picked_a = sb.tile([P, I], F32, name="picked_a", tag="scores1")
        nc.vector.tensor_copy(picked_a[:], scores[0][:].indirect(offsets[:]))
        picked = (picked_a, picked_b)

        logsig = sb.tile([P, 2, I], F32, name="logsig")
        negsp = sb.tile([P, 2, I], F32, name="negsp", tag="negsp")
        prod = sb.tile([P, I], F32, name="prod")
        for hs in halves:
            nc.scalar.activation(logsig[:, :, hs], sig[:, :, hs], ACT.Ln, bias=LN_FLOOR)
        for hs in halves:
            for j in range(2):
                nc.vector.scalar_tensor_tensor(
                    negsp[:, j, hs], picked[j][:, hs], -1.0, logsig[:, j, hs], ALU.mult, ALU.min
                )
        for hs in halves:
            nc.vector.tensor_tensor(prod[:, hs], negsp[:, 0, hs], negsp[:, 1, hs], ALU.mult)

        diff = sb.tile([P, I], F32, name="diff")
        nc.vector.tensor_tensor(diff[:], picked_a[:], picked_b[:], ALU.subtract)
        absdiff = sb.tile([P, I], F32, name="absdiff", tag="negsp")
        nc.vector.scalar_tensor_tensor(absdiff[:], diff[:], -1.0, diff[:], ALU.mult, ALU.max)

        root = sb.tile([P, I], F32, name="root")
        score = sb.tile([P, I], F32, name="score")
        for hs in halves:
            nc.scalar.activation(root[:, hs], prod[:, hs], ACT.Sqrt, bias=0.1)
        for hs in halves:
            nc.vector.scalar_tensor_tensor(
                score[:, hs], root[:, hs], lam_sb[:], absdiff[:, hs], ALU.mult, ALU.subtract
            )
        negmax = sb.tile([P, 1], F32, name="negmax")
        nc.vector.tensor_reduce(negmax[:], score[:], mybir.AxisListType.X, ALU.max, negate=True)
        prob = sb.tile([P, I], F32, name="prob")
        total = sb.tile([P, 1], F32, name="total")
        nc.scalar.activation(prob[:], score[:], ACT.Exp, bias=negmax[:], accum_out=total[:])
        inv = sb.tile([P, 1], F32, name="inv")
        nc.vector.reciprocal(inv[:], total[:])
        ws = sb.tile([P, I], F32, name="ws")
        nc.vector.tensor_scalar(ws[:], prob[:], inv[:], 256.0, ALU.mult, ALU.mult)
        nc.vector.tensor_copy(wf[:].indirect(offsets[:]), ws[:])

        result = sb.tile([P, T], F32, name="result")
        queues = (nc.sync, nc.scalar)
        for n in range(len(STORE_EDGES) - 1):
            cols = slice(STORE_EDGES[n], STORE_EDGES[n + 1])
            nc.vector.scalar_tensor_tensor(
                result[:, cols], old_sb[:, cols], fade_sb[:], wf[:, cols], ALU.mult, ALU.add
            )
            queues[n % 2].dma_start(out=out[:, cols], in_=result[:, cols])
